import numpy as np, ml_dtypes
CORES = [24,26,29,31,48,50,53,55]
N = 8
VB, TK = 1, 128
def setup_inputs(rng):
    h = rng.standard_normal((128, TK), dtype=np.float32) / 4; w = rng.standard_normal((N, 128, VB * 128), dtype=np.float32)
    a = 2 * np.pi * rng.random((TK)); s = 400 * rng.random((TK)) ** 1.5; h[0] = s * np.cos(a); h[1] = s * np.sin(a); h[2] = 150 * rng.standard_normal((TK)); w[:, 2, :] = 1 + w[:, 2, :] / 50
    a = (2 * np.pi * rng.random() + np.pi / 2 * (rng.permutation(N).reshape(N, 1, 1) + 0.5) / N - 0.5 + (np.arange(VB).reshape(1, VB, 1) + rng.random((N, VB, 128))) / VB).reshape(N, VB * 128); w[:, 0, :] = np.cos(a); w[:, 1, :] = np.sin(a)
    tgt = rng.integers(0, N * VB * 128, size=TK)
    oh = np.zeros((N * VB * 128, TK), np.float32); oh[tgt, np.arange(TK)] = 1.0
    oh = oh.reshape(N, VB, 128, TK).transpose(0, 2, 1, 3).reshape(N, 128, VB * TK)
    return {"h": np.broadcast_to(h, (N, 128, TK)).astype(ml_dtypes.bfloat16), "w": w.astype(ml_dtypes.bfloat16), "oh": oh.astype(ml_dtypes.bfloat16)}
def reference(h, w, oh):
    H, W, OH = h.astype(np.float64), w.astype(np.float64), oh.astype(np.float64)
    Z = np.concatenate([W[r].T @ H[r] for r in range(N)], axis=0)
    O = np.concatenate([OH[r][:, TK * b:TK * b + TK] for r in range(N) for b in range(VB)], axis=0)
    m = Z.max(axis=0)
    P = np.exp(Z - m); P = P / P.sum(axis=0)
    G = P - O
    d = sum(W[r] @ G[VB * 128 * r:VB * 128 * (r + 1)] for r in range(N)).astype(ml_dtypes.bfloat16)
    return {"d": np.broadcast_to(d, (N,) + d.shape)}

@@ -1,0 +1,207 @@
+from concourse.bass import DstId, RemoteDMATransfer
+from concourse.mybir import AluOpType, AxisListType, ActivationFunctionType
+
+MSG = 258
+SLOT = 264
+C_T, C_U, C_S, C_C = 0, 128, 256, 257
+NL = 4
+
+SCRATCH = {
+    "h_sb": ("sbuf", [128, 128], "bfloat16"),
+    "w_sb": ("sbuf", [128, 128], "bfloat16"),
+    "oh_sb": ("sbuf", [128, 128], "bfloat16"),
+    "zero": ("sbuf", [128, 8], "float32"),
+    "ones": ("sbuf", [128, 128], "bfloat16"),
+    "ident": ("sbuf", [128, 128], "bfloat16"),
+    "wtx": ("sbuf", [128, 136], "bfloat16"),
+    "et_sb": ("sbuf", [128, 128], "bfloat16"),
+    "e_sb": ("sbuf", [128, 128], "bfloat16"),
+    "land1": ("sbuf", [128, NL * SLOT], "bfloat16"),
+    "buf2": ("sbuf", [128, 2 * SLOT], "bfloat16"),
+    "a1": ("sbuf", [128, NL], "float32"),
+    "dg1": ("sbuf", [128, NL * 128], "bfloat16"),
+    "nc2": ("sbuf", [128, 1], "float32"),
+    "a2": ("sbuf", [128, 2], "float32"),
+    "as2": ("sbuf", [128, 2], "float32"),
+    "s2": ("sbuf", [128, 1], "float32"),
+    "rs2": ("sbuf", [128, 1], "float32"),
+    "dg2": ("sbuf", [128, 256], "bfloat16"),
+    "d_sb": ("sbuf", [128, 128], "bfloat16"),
+    "zt_ps": ("psum", [128, 512], "float32"),
+    "wt_ps": ("psum", [128, 1024], "bfloat16"),
+    "e_ps": ("psum", [128, 1024], "bfloat16"),
+    "tt_ps": ("psum", [128, 512], "float32"),
+    "ut_ps": ("psum", [128, 512], "float32"),
+    "t1_ps": ("psum", [128, 512], "float32"),
+    "u1_ps": ("psum", [128, 512], "float32"),
+    "d_ps": ("psum", [128, 512], "float32"),
+}
+SEMAPHORES = (["ld_w", "ld_h", "ld_oh", "z0", "o1", "idn", "onec", "zt", "wtp", "negc", "wt", "et", "ep", "e", "ttp", "tcp",
+               "utp", "ucp", "nc1", "a1", "t1p", "u1p", "t1c", "u1c", "arr2", "nc2", "a2", "as2", "s2", "rs2", "dg2_0",
+               "dg2_1", "dp", "dsb", "st", "sent"]
+              + ["arr1_%d" % k for k in range(NL)] + ["dg1_%d" % k for k in range(NL)])
+
+
+def _engines(mask):
+    return bin(mask).count("1")
+
+
+def _common_mask(topo, src, dsts):
+    m = topo.mask(src, dsts[0])
+    for d in dsts[1:]:
+        m &= topo.mask(src, d)
+    return m
+
+
+def _carrier(topo, senders, dsts, dst):
+    able = [c for c in senders if topo.may_write(c, dst)]
+    near = [c for c in able if topo.die(c) == topo.die(dst)] or able
+    same = [x for x in dsts if topo.die(x) == topo.die(dst)]
+    return near[same.index(dst) % len(near)]
+
+
+def rank_program(g, core, T, topo):
+    if T.rank_of(core) is None:
+        return
+    S = T.sem
+    V, A, PE, SY = g.vector, g.scalar, g.tensor, g.sync
+    Exp, Copy = ActivationFunctionType.Exp, ActivationFunctionType.Copy
+    X = AxisListType.X
+    mult = AluOpType.mult
+
+    here = [c for c in T.cores if topo.chip(c) == topo.chip(core)]
+    there = [c for c in T.cores if topo.chip(c) != topo.chip(core)]
+    peers = [c for c in here if c != core]
+    me = here.index(core)
+    others = [k for k in range(len(here)) if k != me]
+    far = [d for d in there if _carrier(topo, here, there, d) == core]
+    my_carrier = _carrier(topo, there, here, core)
+    its_far = [d for d in here if _carrier(topo, there, here, d) == my_carrier]
+    n_arr2 = _engines(_common_mask(topo, my_carrier, its_far))
+
+    def n_arr1(k):
+        return _engines(_common_mask(topo, here[k], [c for c in here if c != here[k]]))
+
+    def dst_id(c):
+        rid, pid, _ = topo.addr(c)
+        return DstId(rid=rid, pnc=pid)
+
+    o = me * SLOT
+    ident = T.ident[:]
+
+    SY.dma_start(T.w_sb[:], T.w[:]).then_inc(S.ld_w, 16)
+    A.dma_start(T.h_sb[:], T.h[:]).then_inc(S.ld_h, 16)
+    SY.dma_start(T.oh_sb[:], T.oh[:]).then_inc(S.ld_oh, 16)
+    V.memset(T.zero[:], 0.0).then_inc(S.z0, 1)
+    V.memset(T.ones[:], 1.0).then_inc(S.o1, 1)
+    g.wait_ge(S.o1, 1)
+    g.affine_select(ident, T.ones[:], [[-1, 128]], AluOpType.is_equal, 0.0, 0, 1).then_inc(S.idn, 1)
+    A.wait_ge(S.z0, 1)
+    A.activation(T.wtx[:, 128:129], T.zero[:, 0:1], Exp).then_inc(S.onec, 1)
+
+    PE.wait_ge(S.ld_h, 16)
+    PE.wait_ge(S.ld_w, 16)
+    PE.matmul(T.zt_ps[:, 0:128], T.h_sb[:], T.w_sb[:], True, True).then_inc(S.zt, 1)
+    PE.wait_ge(S.idn, 1)
+    PE.transpose(T.wt_ps[:, 0:128], T.w_sb[:], ident).then_inc(S.wtp, 1)
+    V.wait_ge(S.zt, 1)
+    V.tensor_reduce(T.land1[:, o + C_C:o + C_C + 1], T.zt_ps[:, 0:128], X, AluOpType.max, negate=True).then_inc(S.negc, 1)
+    V.wait_ge(S.wtp, 1)
+    V.tensor_copy(T.wtx[:, 0:128], T.wt_ps[:, 0:128]).then_inc(S.wt, 1)
+    A.wait_ge(S.negc, 1)
+    A.activation(T.et_sb[:], T.zt_ps[:, 0:128], Exp, bias=T.land1[:, o + C_C:o + C_C + 1]).then_inc(S.et, 1)
+    PE.wait_ge(S.et, 1)
+    PE.transpose(T.e_ps[:, 0:128], T.et_sb[:], ident).then_inc(S.ep, 1)
+    PE.wait_ge(S.wt, 1)
+    PE.wait_ge(S.ld_oh, 16)
+    PE.matmul(T.tt_ps[:, 0:128], T.oh_sb[:], T.wtx[:, 0:128], True, True).then_inc(S.ttp, 1)
+    V.wait_ge(S.ep, 1)
+    V.tensor_copy(T.e_sb[:], T.e_ps[:, 0:128]).then_inc(S.e, 1)
+    A.wait_ge(S.ttp, 1)
+    A.activation(T.land1[:, o + C_T:o + C_T + 128], T.tt_ps[:, 0:128], Copy, scale=-1.0).then_inc(S.tcp, 1)
+    PE.wait_ge(S.e, 1)
+    PE.wait_ge(S.onec, 1)
+    PE.matmul(T.ut_ps[:, 0:129], T.e_sb[:], T.wtx[:, 0:129], True, True).then_inc(S.utp, 1)
+    V.wait_ge(S.utp, 1)
+    V.tensor_copy(T.land1[:, o + C_U:o + C_U + 129], T.ut_ps[:, 0:129]).then_inc(S.ucp, 1)
+
+    g.wait_ge(S.negc, 1)
+    g.wait_ge(S.tcp, 1)
+    g.wait_ge(S.ucp, 1)
+    m1 = _common_mask(topo, core, peers)
+    msg = T.land1[:, o:o + MSG]
+    g.remote_dma_fused([RemoteDMATransfer(dst_ids=[dst_id(c) for c in peers], dma_engine_mask=m1,
+                                          remote_sem=S["arr1_%d" % me], srcs=[msg], dsts=[msg for _ in peers], alu_op=0)],
+                       local_sem=S.sent)
+    n_sent = _engines(m1)
+
+    PE.wait_ge(S.tcp, 1)
+    PE.matmul(T.t1_ps[:, 0:128], ident, T.land1[:, o + C_T:o + C_T + 128], True, False)
+    for i, k in enumerate(others):
+        PE.wait_ge(S["arr1_%d" % k], n_arr1(k))
+        mm = PE.matmul(T.t1_ps[:, 0:128], ident, T.land1[:, k * SLOT + C_T:k * SLOT + C_T + 128], False, i == len(others) - 1)
+    mm.then_inc(S.t1p, 1)
+    for k in others:
+        V.wait_ge(S["arr1_%d" % k], n_arr1(k))
+        A.wait_ge(S["arr1_%d" % k], n_arr1(k))
+    V.wait_ge(S.negc, 1)
+    V.tensor_reduce(T.buf2[:, C_C:C_C + 1], T.land1[:, C_C::SLOT], X, AluOpType.min).then_inc(S.nc1, 1)
+    A.wait_ge(S.nc1, 1)
+    A.activation(T.a1[:], T.land1[:, C_C::SLOT], Exp, bias=T.buf2[:, C_C:C_C + 1], scale=-1.0).then_inc(S.a1, 1)
+    V.wait_ge(S.a1, 1)
+    V.wait_ge(S.idn, 1)
+    for k in range(len(here)):
+        V.tensor_scalar(T.dg1[:, k * 128:(k + 1) * 128], ident, T.a1[:, k:k + 1], None, mult).then_inc(S["dg1_%d" % k], 1)
+    A.wait_ge(S.t1p, 1)
+    A.activation(T.buf2[:, C_T:C_T + 128], T.t1_ps[:, 0:128], Copy).then_inc(S.t1c, 1)
+    PE.wait_ge(S.ucp, 1)
+    for k in range(len(here)):
+        PE.wait_ge(S["dg1_%d" % k], 1)
+        mm = PE.matmul(T.u1_ps[:, 0:129], T.dg1[:, k * 128:(k + 1) * 128], T.land1[:, k * SLOT + C_U:k * SLOT + C_U + 129],
+                       k == 0, k == len(here) - 1)
+    mm.then_inc(S.u1p, 1)
+    V.wait_ge(S.u1p, 1)
+    V.tensor_copy(T.buf2[:, C_U:C_U + 129], T.u1_ps[:, 0:129]).then_inc(S.u1c, 1)
+
+    if far:
+        g.wait_ge(S.nc1, 1)
+        g.wait_ge(S.t1c, 1)
+        g.wait_ge(S.u1c, 1)
+        m2 = _common_mask(topo, core, far)
+        g.remote_dma_fused([RemoteDMATransfer(dst_ids=[dst_id(c) for c in far], dma_engine_mask=m2, remote_sem=S.arr2,
+                                              srcs=[T.buf2[:, 0:MSG]], dsts=[T.buf2[:, SLOT:SLOT + MSG] for _ in far],
+                                              alu_op=0)], local_sem=S.sent)
+        n_sent += _engines(m2)
+
+    PE.wait_ge(S.t1c, 1)
+    PE.matmul(T.d_ps[:, 0:128], T.buf2[:, C_T:C_T + 128], ident, True, False)
+    PE.wait_ge(S.arr2, n_arr2)
+    PE.matmul(T.d_ps[:, 0:128], T.buf2[:, SLOT + C_T:SLOT + C_T + 128], ident, False, False)
+    V.wait_ge(S.arr2, n_arr2)
+    V.wait_ge(S.nc1, 1)
+    V.tensor_reduce(T.nc2[:], T.buf2[:, C_C::SLOT], X, AluOpType.min).then_inc(S.nc2, 1)
+    A.wait_ge(S.arr2, n_arr2)
+    A.wait_ge(S.nc2, 1)
+    A.activation(T.a2[:], T.buf2[:, C_C::SLOT], Exp, bias=T.nc2[:], scale=-1.0).then_inc(S.a2, 1)
+    V.wait_ge(S.a2, 1)
+    V.wait_ge(S.u1c, 1)
+    V.tensor_tensor(T.as2[:], T.a2[:], T.buf2[:, C_S::SLOT], mult).then_inc(S.as2, 1)
+    V.wait_ge(S.as2, 1)
+    V.tensor_reduce(T.s2[:], T.as2[:], X, AluOpType.add).then_inc(S.s2, 1)
+    V.wait_ge(S.s2, 1)
+    V.reciprocal(T.rs2[:], T.s2[:]).then_inc(S.rs2, 1)
+    V.wait_ge(S.rs2, 1)
+    for j in range(2):
+        V.tensor_scalar(T.dg2[:, j * 128:(j + 1) * 128], ident, T.a2[:, j:j + 1], T.rs2[:], mult, mult).then_inc(S["dg2_%d" % j], 1)
+    PE.wait_ge(S.u1c, 1)
+    for j in range(2):
+        PE.wait_ge(S["dg2_%d" % j], 1)
+        mm = PE.matmul(T.d_ps[:, 0:128], T.buf2[:, j * SLOT + C_U:j * SLOT + C_U + 128], T.dg2[:, j * 128:(j + 1) * 128],
+                       False, j == 1)
+    mm.then_inc(S.dp, 1)
+    V.wait_ge(S.dp, 1)
+    V.tensor_copy(T.d_sb[:], T.d_ps[:, 0:128]).then_inc(S.dsb, 1)
+    SY.wait_ge(S.dsb, 1)
+    SY.dma_start(T.d[:], T.d_sb[:]).then_inc(S.st, 16)
+    SY.wait_ge(S.st, 16)
+    g.wait_ge(S.sent, n_sent)

@@ -1,24 +1,31 @@
 from concourse.bass import DstId, RemoteDMATransfer
 from concourse.mybir import AluOpType, AxisListType, ActivationFunctionType
 
-MSG = 258
-SLOT = 264
-C_T, C_U, C_S, C_C = 0, 128, 256, 257
 NL = 4
+WA = 130
+SA = 136
+A_S, A_C = 128, 129
+SB = 128
+S2 = 4
+W2 = 256
 
 SCRATCH = {
     "h_sb": ("sbuf", [128, 128], "bfloat16"),
     "w_sb": ("sbuf", [128, 128], "bfloat16"),
     "oh_sb": ("sbuf", [128, 128], "bfloat16"),
-    "zero": ("sbuf", [128, 8], "float32"),
+    "zero": ("sbuf", [128, 128], "bfloat16"),
     "ones": ("sbuf", [128, 128], "bfloat16"),
     "ident": ("sbuf", [128, 128], "bfloat16"),
-    "wtx": ("sbuf", [128, 136], "bfloat16"),
+    "wt_sb": ("sbuf", [128, 128], "bfloat16"),
     "et_sb": ("sbuf", [128, 128], "bfloat16"),
     "e_sb": ("sbuf", [128, 128], "bfloat16"),
-    "land1": ("sbuf", [128, NL * SLOT], "bfloat16"),
-    "buf2": ("sbuf", [128, 2 * SLOT], "bfloat16"),
+    "s32": ("sbuf", [128, 1], "float32"),
+    "la": ("sbuf", [128, NL * SA], "bfloat16"),
+    "lb": ("sbuf", [128, NL * SB], "bfloat16"),
+    "st2": ("sbuf", [128, 2 * S2], "float32"),
+    "tu2": ("sbuf", [128, 2 * W2], "bfloat16"),
     "a1": ("sbuf", [128, NL], "float32"),
+    "as1": ("sbuf", [128, NL], "float32"),
     "dg1": ("sbuf", [128, NL * 128], "bfloat16"),
     "nc2": ("sbuf", [128, 1], "float32"),
     "a2": ("sbuf", [128, 2], "float32"),
@@ -36,10 +43,10 @@ SCRATCH = {
     "u1_ps": ("psum", [128, 512], "float32"),
     "d_ps": ("psum", [128, 512], "float32"),
 }
-SEMAPHORES = (["ld_w", "ld_h", "ld_oh", "z0", "o1", "idn", "onec", "zt", "wtp", "negc", "wt", "et", "ep", "e", "ttp", "tcp",
-               "utp", "ucp", "nc1", "a1", "t1p", "u1p", "t1c", "u1c", "arr2", "nc2", "a2", "as2", "s2", "rs2", "dg2_0",
-               "dg2_1", "dp", "dsb", "st", "sent"]
-              + ["arr1_%d" % k for k in range(NL)] + ["dg1_%d" % k for k in range(NL)])
+SEMAPHORES = (["ld_w", "ld_h", "ld_oh", "z0", "o1", "idn", "zt", "wtp", "negc", "wt", "et", "scp", "ep", "e", "ttp", "tcp",
+               "utp", "ucp", "nc1", "a1", "as1", "s1", "t1p", "u1p", "t1c", "u1c", "arr2a", "arr2b", "nc2", "a2", "as2", "s2",
+               "rs2", "dg2_0", "dg2_1", "dp", "dsb", "st", "sent"]
+              + ["arra_%d" % k for k in range(NL)] + ["arrb_%d" % k for k in range(NL)] + ["dg1_%d" % k for k in range(NL)])
 
 
 def _engines(mask):
@@ -82,22 +89,27 @@ def rank_program(g, core, T, topo):
     def n_arr1(k):
         return _engines(_common_mask(topo, here[k], [c for c in here if c != here[k]]))
 
-    def dst_id(c):
-        rid, pid, _ = topo.addr(c)
-        return DstId(rid=rid, pnc=pid)
+    def send(dsts, mask, sem, src, dst):
+        ids = []
+        for c in dsts:
+            rid, pid, _ = topo.addr(c)
+            ids.append(DstId(rid=rid, pnc=pid))
+        g.remote_dma_fused([RemoteDMATransfer(dst_ids=ids, dma_engine_mask=mask, remote_sem=sem, srcs=[src],
+                                              dsts=[dst for _ in dsts], alu_op=0)], local_sem=S.sent)
+        return _engines(mask)
 
-    o = me * SLOT
+    oa, ob = me * SA, me * SB
     ident = T.ident[:]
+    negc = T.la[:, oa + A_C:oa + A_C + 1]
 
     SY.dma_start(T.w_sb[:], T.w[:]).then_inc(S.ld_w, 16)
     A.dma_start(T.h_sb[:], T.h[:]).then_inc(S.ld_h, 16)
     SY.dma_start(T.oh_sb[:], T.oh[:]).then_inc(S.ld_oh, 16)
     V.memset(T.zero[:], 0.0).then_inc(S.z0, 1)
-    V.memset(T.ones[:], 1.0).then_inc(S.o1, 1)
+    A.wait_ge(S.z0, 1)
+    A.activation(T.ones[:], T.zero[:], Exp).then_inc(S.o1, 1)
     g.wait_ge(S.o1, 1)
     g.affine_select(ident, T.ones[:], [[-1, 128]], AluOpType.is_equal, 0.0, 0, 1).then_inc(S.idn, 1)
-    A.wait_ge(S.z0, 1)
-    A.activation(T.wtx[:, 128:129], T.zero[:, 0:1], Exp).then_inc(S.onec, 1)
 
     PE.wait_ge(S.ld_h, 16)
     PE.wait_ge(S.ld_w, 16)
@@ -105,87 +117,89 @@ def rank_program(g, core, T, topo):
     PE.wait_ge(S.idn, 1)
     PE.transpose(T.wt_ps[:, 0:128], T.w_sb[:], ident).then_inc(S.wtp, 1)
     V.wait_ge(S.zt, 1)
-    V.tensor_reduce(T.land1[:, o + C_C:o + C_C + 1], T.zt_ps[:, 0:128], X, AluOpType.max, negate=True).then_inc(S.negc, 1)
+    V.tensor_reduce(negc, T.zt_ps[:, 0:128], X, AluOpType.max, negate=True).then_inc(S.negc, 1)
     V.wait_ge(S.wtp, 1)
-    V.tensor_copy(T.wtx[:, 0:128], T.wt_ps[:, 0:128]).then_inc(S.wt, 1)
+    V.tensor_copy(T.wt_sb[:], T.wt_ps[:, 0:128]).then_inc(S.wt, 1)
     A.wait_ge(S.negc, 1)
-    A.activation(T.et_sb[:], T.zt_ps[:, 0:128], Exp, bias=T.land1[:, o + C_C:o + C_C + 1]).then_inc(S.et, 1)
-    PE.wait_ge(S.et, 1)
-    PE.transpose(T.e_ps[:, 0:128], T.et_sb[:], ident).then_inc(S.ep, 1)
+    A.activation(T.et_sb[:], T.zt_ps[:, 0:128], Exp, bias=negc, accum_out=T.s32[:]).then_inc(S.et, 1)
     PE.wait_ge(S.wt, 1)
     PE.wait_ge(S.ld_oh, 16)
-    PE.matmul(T.tt_ps[:, 0:128], T.oh_sb[:], T.wtx[:, 0:128], True, True).then_inc(S.ttp, 1)
+    PE.matmul(T.tt_ps[:, 0:128], T.oh_sb[:], T.wt_sb[:], True, True).then_inc(S.ttp, 1)
+    PE.wait_ge(S.et, 1)
+    PE.transpose(T.e_ps[:, 0:128], T.et_sb[:], ident).then_inc(S.ep, 1)
+    V.wait_ge(S.et, 1)
+    V.tensor_copy(T.la[:, oa + A_S:oa + A_S + 1], T.s32[:]).then_inc(S.scp, 1)
+    A.wait_ge(S.ttp, 1)
+    A.activation(T.la[:, oa:oa + 128], T.tt_ps[:, 0:128], Copy, scale=-1.0).then_inc(S.tcp, 1)
     V.wait_ge(S.ep, 1)
     V.tensor_copy(T.e_sb[:], T.e_ps[:, 0:128]).then_inc(S.e, 1)
-    A.wait_ge(S.ttp, 1)
-    A.activation(T.land1[:, o + C_T:o + C_T + 128], T.tt_ps[:, 0:128], Copy, scale=-1.0).then_inc(S.tcp, 1)
     PE.wait_ge(S.e, 1)
-    PE.wait_ge(S.onec, 1)
-    PE.matmul(T.ut_ps[:, 0:129], T.e_sb[:], T.wtx[:, 0:129], True, True).then_inc(S.utp, 1)
+    PE.matmul(T.ut_ps[:, 0:128], T.e_sb[:], T.wt_sb[:], True, True).then_inc(S.utp, 1)
     V.wait_ge(S.utp, 1)
-    V.tensor_copy(T.land1[:, o + C_U:o + C_U + 129], T.ut_ps[:, 0:129]).then_inc(S.ucp, 1)
+    V.tensor_copy(T.lb[:, ob:ob + SB], T.ut_ps[:, 0:128]).then_inc(S.ucp, 1)
 
-    g.wait_ge(S.negc, 1)
-    g.wait_ge(S.tcp, 1)
-    g.wait_ge(S.ucp, 1)
     m1 = _common_mask(topo, core, peers)
-    msg = T.land1[:, o:o + MSG]
-    g.remote_dma_fused([RemoteDMATransfer(dst_ids=[dst_id(c) for c in peers], dma_engine_mask=m1,
-                                          remote_sem=S["arr1_%d" % me], srcs=[msg], dsts=[msg for _ in peers], alu_op=0)],
-                       local_sem=S.sent)
-    n_sent = _engines(m1)
+    g.wait_ge(S.negc, 1)
+    g.wait_ge(S.scp, 1)
+    g.wait_ge(S.tcp, 1)
+    n_sent = send(peers, m1, S["arra_%d" % me], T.la[:, oa:oa + WA], T.la[:, oa:oa + WA])
+    g.wait_ge(S.ucp, 1)
+    n_sent += send(peers, m1, S["arrb_%d" % me], T.lb[:, ob:ob + SB], T.lb[:, ob:ob + SB])
 
     PE.wait_ge(S.tcp, 1)
-    PE.matmul(T.t1_ps[:, 0:128], ident, T.land1[:, o + C_T:o + C_T + 128], True, False)
+    PE.matmul(T.t1_ps[:, 0:128], ident, T.la[:, oa:oa + 128], True, False)
     for i, k in enumerate(others):
-        PE.wait_ge(S["arr1_%d" % k], n_arr1(k))
-        mm = PE.matmul(T.t1_ps[:, 0:128], ident, T.land1[:, k * SLOT + C_T:k * SLOT + C_T + 128], False, i == len(others) - 1)
+        PE.wait_ge(S["arra_%d" % k], n_arr1(k))
+        mm = PE.matmul(T.t1_ps[:, 0:128], ident, T.la[:, k * SA:k * SA + 128], False, i == len(others) - 1)
     mm.then_inc(S.t1p, 1)
     for k in others:
-        V.wait_ge(S["arr1_%d" % k], n_arr1(k))
-        A.wait_ge(S["arr1_%d" % k], n_arr1(k))
+        V.wait_ge(S["arra_%d" % k], n_arr1(k))
+        A.wait_ge(S["arra_%d" % k], n_arr1(k))
     V.wait_ge(S.negc, 1)
-    V.tensor_reduce(T.buf2[:, C_C:C_C + 1], T.land1[:, C_C::SLOT], X, AluOpType.min).then_inc(S.nc1, 1)
+    V.wait_ge(S.scp, 1)
+    V.tensor_reduce(T.st2[:, 1:2], T.la[:, A_C::SA], X, AluOpType.min).then_inc(S.nc1, 1)
     A.wait_ge(S.nc1, 1)
-    A.activation(T.a1[:], T.land1[:, C_C::SLOT], Exp, bias=T.buf2[:, C_C:C_C + 1], scale=-1.0).then_inc(S.a1, 1)
+    A.activation(T.a1[:], T.la[:, A_C::SA], Exp, bias=T.st2[:, 1:2], scale=-1.0).then_inc(S.a1, 1)
     V.wait_ge(S.a1, 1)
+    V.tensor_tensor(T.as1[:], T.a1[:], T.la[:, A_S::SA], mult).then_inc(S.as1, 1)
+    V.wait_ge(S.as1, 1)
+    V.tensor_reduce(T.st2[:, 0:1], T.as1[:], X, AluOpType.add).then_inc(S.s1, 1)
     V.wait_ge(S.idn, 1)
-    for k in range(len(here)):
+    for k in [me] + others:
         V.tensor_scalar(T.dg1[:, k * 128:(k + 1) * 128], ident, T.a1[:, k:k + 1], None, mult).then_inc(S["dg1_%d" % k], 1)
     A.wait_ge(S.t1p, 1)
-    A.activation(T.buf2[:, C_T:C_T + 128], T.t1_ps[:, 0:128], Copy).then_inc(S.t1c, 1)
-    PE.wait_ge(S.ucp, 1)
-    for k in range(len(here)):
-        PE.wait_ge(S["dg1_%d" % k], 1)
-        mm = PE.matmul(T.u1_ps[:, 0:129], T.dg1[:, k * 128:(k + 1) * 128], T.land1[:, k * SLOT + C_U:k * SLOT + C_U + 129],
-                       k == 0, k == len(here) - 1)
-    mm.then_inc(S.u1p, 1)
-    V.wait_ge(S.u1p, 1)
-    V.tensor_copy(T.buf2[:, C_U:C_U + 129], T.u1_ps[:, 0:129]).then_inc(S.u1c, 1)
+    A.activation(T.tu2[:, 0:128], T.t1_ps[:, 0:128], Copy).then_inc(S.t1c, 1)
 
     if far:
+        m2 = _common_mask(topo, core, far)
         g.wait_ge(S.nc1, 1)
+        g.wait_ge(S.s1, 1)
+        n_sent += send(far, m2, S.arr2a, T.st2[:, 0:2], T.st2[:, S2:S2 + 2])
+
+    PE.wait_ge(S.ucp, 1)
+    for i, k in enumerate([me] + others):
+        if k != me:
+            PE.wait_ge(S["arrb_%d" % k], n_arr1(k))
+        PE.wait_ge(S["dg1_%d" % k], 1)
+        mm = PE.matmul(T.u1_ps[:, 0:128], T.dg1[:, k * 128:(k + 1) * 128], T.lb[:, k * SB:(k + 1) * SB], i == 0, i == len(others))
+    mm.then_inc(S.u1p, 1)
+    V.wait_ge(S.u1p, 1)
+    V.tensor_copy(T.tu2[:, 128:256], T.u1_ps[:, 0:128]).then_inc(S.u1c, 1)
+
+    if far:
         g.wait_ge(S.t1c, 1)
         g.wait_ge(S.u1c, 1)
-        m2 = _common_mask(topo, core, far)
-        g.remote_dma_fused([RemoteDMATransfer(dst_ids=[dst_id(c) for c in far], dma_engine_mask=m2, remote_sem=S.arr2,
-                                              srcs=[T.buf2[:, 0:MSG]], dsts=[T.buf2[:, SLOT:SLOT + MSG] for _ in far],
-                                              alu_op=0)], local_sem=S.sent)
-        n_sent += _engines(m2)
+        n_sent += send(far, m2, S.arr2b, T.tu2[:, 0:W2], T.tu2[:, W2:2 * W2])
 
-    PE.wait_ge(S.t1c, 1)
-    PE.matmul(T.d_ps[:, 0:128], T.buf2[:, C_T:C_T + 128], ident, True, False)
-    PE.wait_ge(S.arr2, n_arr2)
-    PE.matmul(T.d_ps[:, 0:128], T.buf2[:, SLOT + C_T:SLOT + C_T + 128], ident, False, False)
-    V.wait_ge(S.arr2, n_arr2)
+    V.wait_ge(S.arr2a, n_arr2)
     V.wait_ge(S.nc1, 1)
-    V.tensor_reduce(T.nc2[:], T.buf2[:, C_C::SLOT], X, AluOpType.min).then_inc(S.nc2, 1)
-    A.wait_ge(S.arr2, n_arr2)
+    V.wait_ge(S.s1, 1)
+    V.tensor_reduce(T.nc2[:], T.st2[:, 1::S2], X, AluOpType.min).then_inc(S.nc2, 1)
+    A.wait_ge(S.arr2a, n_arr2)
     A.wait_ge(S.nc2, 1)
-    A.activation(T.a2[:], T.buf2[:, C_C::SLOT], Exp, bias=T.nc2[:], scale=-1.0).then_inc(S.a2, 1)
+    A.activation(T.a2[:], T.st2[:, 1::S2], Exp, bias=T.nc2[:], scale=-1.0).then_inc(S.a2, 1)
     V.wait_ge(S.a2, 1)
-    V.wait_ge(S.u1c, 1)
-    V.tensor_tensor(T.as2[:], T.a2[:], T.buf2[:, C_S::SLOT], mult).then_inc(S.as2, 1)
+    V.tensor_tensor(T.as2[:], T.a2[:], T.st2[:, 0::S2], mult).then_inc(S.as2, 1)
     V.wait_ge(S.as2, 1)
     V.tensor_reduce(T.s2[:], T.as2[:], X, AluOpType.add).then_inc(S.s2, 1)
     V.wait_ge(S.s2, 1)
@@ -193,12 +207,16 @@ def rank_program(g, core, T, topo):
     V.wait_ge(S.rs2, 1)
     for j in range(2):
         V.tensor_scalar(T.dg2[:, j * 128:(j + 1) * 128], ident, T.a2[:, j:j + 1], T.rs2[:], mult, mult).then_inc(S["dg2_%d" % j], 1)
+
+    PE.wait_ge(S.t1c, 1)
+    PE.matmul(T.d_ps[:, 0:128], T.tu2[:, 0:128], ident, True, False)
     PE.wait_ge(S.u1c, 1)
-    for j in range(2):
-        PE.wait_ge(S["dg2_%d" % j], 1)
-        mm = PE.matmul(T.d_ps[:, 0:128], T.buf2[:, j * SLOT + C_U:j * SLOT + C_U + 128], T.dg2[:, j * 128:(j + 1) * 128],
-                       False, j == 1)
-    mm.then_inc(S.dp, 1)
+    PE.wait_ge(S.dg2_0, 1)
+    PE.matmul(T.d_ps[:, 0:128], T.tu2[:, 128:256], T.dg2[:, 0:128], False, False)
+    PE.wait_ge(S.arr2b, n_arr2)
+    PE.matmul(T.d_ps[:, 0:128], T.tu2[:, W2:W2 + 128], ident, False, False)
+    PE.wait_ge(S.dg2_1, 1)
+    PE.matmul(T.d_ps[:, 0:128], T.tu2[:, W2 + 128:W2 + 256], T.dg2[:, 128:256], False, True).then_inc(S.dp, 1)
     V.wait_ge(S.dp, 1)
     V.tensor_copy(T.d_sb[:], T.d_ps[:, 0:128]).then_inc(S.dsb, 1)
     SY.wait_ge(S.dsb, 1)

@@ -13,7 +13,8 @@ SCRATCH = {
     "h_sb": ("sbuf", [128, 128], "bfloat16"),
     "w_sb": ("sbuf", [128, 128], "bfloat16"),
     "oh_sb": ("sbuf", [128, 128], "bfloat16"),
-    "zero": ("sbuf", [128, 128], "bfloat16"),
+    "zero": ("sbuf", [128, 1], "float32"),
+    "unit": ("sbuf", [128, 1], "float32"),
     "ones": ("sbuf", [128, 128], "bfloat16"),
     "ident": ("sbuf", [128, 128], "bfloat16"),
     "wt_sb": ("sbuf", [128, 128], "bfloat16"),
@@ -43,7 +44,7 @@ SCRATCH = {
     "u1_ps": ("psum", [128, 512], "float32"),
     "d_ps": ("psum", [128, 512], "float32"),
 }
-SEMAPHORES = (["ld_w", "ld_h", "ld_oh", "z0", "o1", "idn", "zt", "wtp", "negc", "wt", "et", "scp", "ep", "e", "ttp", "tcp",
+SEMAPHORES = (["ld_w", "ld_h", "ld_oh", "z0", "un", "o1", "idn", "zt", "wtp", "negc", "wt", "et", "scp", "ep", "e", "ttp", "tcp",
                "utp", "ucp", "nc1", "a1", "as1", "s1", "t1p", "u1p", "t1c", "u1c", "arr2a", "arr2b", "nc2", "a2", "as2", "s2",
                "rs2", "dg2_0", "dg2_1", "dp", "dsb", "st", "sent"]
               + ["arra_%d" % k for k in range(NL)] + ["arrb_%d" % k for k in range(NL)] + ["dg1_%d" % k for k in range(NL)])
@@ -78,9 +79,10 @@ def rank_program(g, core, T, topo):
 
     here = [c for c in T.cores if topo.chip(c) == topo.chip(core)]
     there = [c for c in T.cores if topo.chip(c) != topo.chip(core)]
-    peers = [c for c in here if c != core]
     me = here.index(core)
     others = [k for k in range(len(here)) if k != me]
+    carriers = [_carrier(topo, here, there, d) for d in there]
+    peers = sorted([c for c in here if c != core], key=lambda c: (c not in carriers, topo.die(c) != topo.die(core)))
     far = [d for d in there if _carrier(topo, here, there, d) == core]
     my_carrier = _carrier(topo, there, here, core)
     its_far = [d for d in here if _carrier(topo, there, here, d) == my_carrier]
@@ -106,8 +108,9 @@ def rank_program(g, core, T, topo):
     A.dma_start(T.h_sb[:], T.h[:]).then_inc(S.ld_h, 16)
     SY.dma_start(T.oh_sb[:], T.oh[:]).then_inc(S.ld_oh, 16)
     V.memset(T.zero[:], 0.0).then_inc(S.z0, 1)
+    V.memset(T.ones[:], 1.0).then_inc(S.o1, 1)
     A.wait_ge(S.z0, 1)
-    A.activation(T.ones[:], T.zero[:], Exp).then_inc(S.o1, 1)
+    A.activation(T.unit[:], T.zero[:], Exp).then_inc(S.un, 1)
     g.wait_ge(S.o1, 1)
     g.affine_select(ident, T.ones[:], [[-1, 128]], AluOpType.is_equal, 0.0, 0, 1).then_inc(S.idn, 1)
 
@@ -128,7 +131,8 @@ def rank_program(g, core, T, topo):
     PE.wait_ge(S.et, 1)
     PE.transpose(T.e_ps[:, 0:128], T.et_sb[:], ident).then_inc(S.ep, 1)
     V.wait_ge(S.et, 1)
-    V.tensor_copy(T.la[:, oa + A_S:oa + A_S + 1], T.s32[:]).then_inc(S.scp, 1)
+    V.wait_ge(S.un, 1)
+    V.tensor_scalar(T.la[:, oa + A_S:oa + A_S + 1], T.s32[:], T.unit[:], None, mult).then_inc(S.scp, 1)
     A.wait_ge(S.ttp, 1)
     A.activation(T.la[:, oa:oa + 128], T.tt_ps[:, 0:128], Copy, scale=-1.0).then_inc(S.tcp, 1)
     V.wait_ge(S.ep, 1)

from concourse.bass import DstId, RemoteDMATransfer
from concourse.mybir import AluOpType, AxisListType, ActivationFunctionType

NL = 4
WA = 130
SA = 136
A_S, A_C = 128, 129
SB = 128
S2 = 4
W2 = 256

SCRATCH = {
    "h_sb": ("sbuf", [128, 128], "bfloat16"),
    "w_sb": ("sbuf", [128, 128], "bfloat16"),
    "oh_sb": ("sbuf", [128, 128], "bfloat16"),
    "zero": ("sbuf", [128, 1], "float32"),
    "unit": ("sbuf", [128, 1], "float32"),
    "ones": ("sbuf", [128, 128], "bfloat16"),
    "ident": ("sbuf", [128, 128], "bfloat16"),
    "wt_sb": ("sbuf", [128, 128], "bfloat16"),
    "et_sb": ("sbuf", [128, 128], "bfloat16"),
    "e_sb": ("sbuf", [128, 128], "bfloat16"),
    "s32": ("sbuf", [128, 1], "float32"),
    "la": ("sbuf", [128, NL * SA], "bfloat16"),
    "lb": ("sbuf", [128, NL * SB], "bfloat16"),
    "st2": ("sbuf", [128, 2 * S2], "float32"),
    "tu2": ("sbuf", [128, 2 * W2], "bfloat16"),
    "a1": ("sbuf", [128, NL], "float32"),
    "as1": ("sbuf", [128, NL], "float32"),
    "dg1": ("sbuf", [128, NL * 128], "bfloat16"),
    "nc2": ("sbuf", [128, 1], "float32"),
    "a2": ("sbuf", [128, 2], "float32"),
    "as2": ("sbuf", [128, 2], "float32"),
    "s2": ("sbuf", [128, 1], "float32"),
    "rs2": ("sbuf", [128, 1], "float32"),
    "dg2": ("sbuf", [128, 256], "bfloat16"),
    "d_sb": ("sbuf", [128, 128], "bfloat16"),
    "zt_ps": ("psum", [128, 512], "float32"),
    "wt_ps": ("psum", [128, 1024], "bfloat16"),
    "e_ps": ("psum", [128, 1024], "bfloat16"),
    "tt_ps": ("psum", [128, 512], "float32"),
    "ut_ps": ("psum", [128, 512], "float32"),
    "t1_ps": ("psum", [128, 512], "float32"),
    "u1_ps": ("psum", [128, 512], "float32"),
    "d_ps": ("psum", [128, 512], "float32"),
}
SEMAPHORES = (["ld_w", "ld_h", "ld_oh", "z0", "un", "o1", "idn", "zt", "wtp", "negc", "wt", "et", "scp", "ep", "e", "ttp", "tcp",
               "utp", "ucp", "nc1", "a1", "as1", "s1", "t1p", "u1p", "t1c", "u1c", "arr2a", "arr2b", "nc2", "a2", "as2", "s2",
               "rs2", "dg2_0", "dg2_1", "dp", "dsb", "st", "sent"]
              + ["arra_%d" % k for k in range(NL)] + ["arrb_%d" % k for k in range(NL)] + ["dg1_%d" % k for k in range(NL)])


def _engines(mask):
    return bin(mask).count("1")


def _common_mask(topo, src, dsts):
    m = topo.mask(src, dsts[0])
    for d in dsts[1:]:
        m &= topo.mask(src, d)
    return m


def _carrier(topo, senders, dsts, dst):
    able = [c for c in senders if topo.may_write(c, dst)]
    near = [c for c in able if topo.die(c) == topo.die(dst)] or able
    same = [x for x in dsts if topo.die(x) == topo.die(dst)]
    return near[same.index(dst) % len(near)]


def rank_program(g, core, T, topo):
    if T.rank_of(core) is None:
        return
    S = T.sem
    V, A, PE, SY = g.vector, g.scalar, g.tensor, g.sync
    Exp, Copy = ActivationFunctionType.Exp, ActivationFunctionType.Copy
    X = AxisListType.X
    mult = AluOpType.mult

    here = [c for c in T.cores if topo.chip(c) == topo.chip(core)]
    there = [c for c in T.cores if topo.chip(c) != topo.chip(core)]
    me = here.index(core)
    others = [k for k in range(len(here)) if k != me]
    carriers = [_carrier(topo, here, there, d) for d in there]
    peers = sorted([c for c in here if c != core], key=lambda c: (c not in carriers, topo.die(c) != topo.die(core)))
    far = [d for d in there if _carrier(topo, here, there, d) == core]
    my_carrier = _carrier(topo, there, here, core)
    its_far = [d for d in here if _carrier(topo, there, here, d) == my_carrier]
    n_arr2 = _engines(_common_mask(topo, my_carrier, its_far))

    def n_arr1(k):
        return _engines(_common_mask(topo, here[k], [c for c in here if c != here[k]]))

    def send(dsts, mask, sem, src, dst):
        ids = []
        for c in dsts:
            rid, pid, _ = topo.addr(c)
            ids.append(DstId(rid=rid, pnc=pid))
        g.remote_dma_fused([RemoteDMATransfer(dst_ids=ids, dma_engine_mask=mask, remote_sem=sem, srcs=[src],
                                              dsts=[dst for _ in dsts], alu_op=0)], local_sem=S.sent)
        return _engines(mask)

    oa, ob = me * SA, me * SB
    ident = T.ident[:]
    negc = T.la[:, oa + A_C:oa + A_C + 1]

    SY.dma_start(T.w_sb[:], T.w[:]).then_inc(S.ld_w, 16)
    A.dma_start(T.h_sb[:], T.h[:]).then_inc(S.ld_h, 16)
    SY.dma_start(T.oh_sb[:], T.oh[:]).then_inc(S.ld_oh, 16)
    V.memset(T.zero[:], 0.0).then_inc(S.z0, 1)
    V.memset(T.ones[:], 1.0).then_inc(S.o1, 1)
    A.wait_ge(S.z0, 1)
    A.activation(T.unit[:], T.zero[:], Exp).then_inc(S.un, 1)
    g.wait_ge(S.o1, 1)
    g.affine_select(ident, T.ones[:], [[-1, 128]], AluOpType.is_equal, 0.0, 0, 1).then_inc(S.idn, 1)

    PE.wait_ge(S.ld_h, 16)
    PE.wait_ge(S.ld_w, 16)
    PE.matmul(T.zt_ps[:, 0:128], T.h_sb[:], T.w_sb[:], True, True).then_inc(S.zt, 1)
    PE.wait_ge(S.idn, 1)
    PE.transpose(T.wt_ps[:, 0:128], T.w_sb[:], ident).then_inc(S.wtp, 1)
    V.wait_ge(S.zt, 1)
    V.tensor_reduce(negc, T.zt_ps[:, 0:128], X, AluOpType.max, negate=True).then_inc(S.negc, 1)
    V.wait_ge(S.wtp, 1)
    V.tensor_copy(T.wt_sb[:], T.wt_ps[:, 0:128]).then_inc(S.wt, 1)
    A.wait_ge(S.negc, 1)
    A.activation(T.et_sb[:], T.zt_ps[:, 0:128], Exp, bias=negc, accum_out=T.s32[:]).then_inc(S.et, 1)
    PE.wait_ge(S.wt, 1)
    PE.wait_ge(S.ld_oh, 16)
    PE.matmul(T.tt_ps[:, 0:128], T.oh_sb[:], T.wt_sb[:], True, True).then_inc(S.ttp, 1)
    PE.wait_ge(S.et, 1)
    PE.transpose(T.e_ps[:, 0:128], T.et_sb[:], ident).then_inc(S.ep, 1)
    V.wait_ge(S.et, 1)
    V.wait_ge(S.un, 1)
    V.tensor_scalar(T.la[:, oa + A_S:oa + A_S + 1], T.s32[:], T.unit[:], None, mult).then_inc(S.scp, 1)
    A.wait_ge(S.ttp, 1)
    A.activation(T.la[:, oa:oa + 128], T.tt_ps[:, 0:128], Copy, scale=-1.0).then_inc(S.tcp, 1)
    V.wait_ge(S.ep, 1)
    V.tensor_copy(T.e_sb[:], T.e_ps[:, 0:128]).then_inc(S.e, 1)
    PE.wait_ge(S.e, 1)
    PE.matmul(T.ut_ps[:, 0:128], T.e_sb[:], T.wt_sb[:], True, True).then_inc(S.utp, 1)
    V.wait_ge(S.utp, 1)
    V.tensor_copy(T.lb[:, ob:ob + SB], T.ut_ps[:, 0:128]).then_inc(S.ucp, 1)

    m1 = _common_mask(topo, core, peers)
    g.wait_ge(S.negc, 1)
    g.wait_ge(S.scp, 1)
    g.wait_ge(S.tcp, 1)
    n_sent = send(peers, m1, S["arra_%d" % me], T.la[:, oa:oa + WA], T.la[:, oa:oa + WA])
    g.wait_ge(S.ucp, 1)
    n_sent += send(peers, m1, S["arrb_%d" % me], T.lb[:, ob:ob + SB], T.lb[:, ob:ob + SB])

    PE.wait_ge(S.tcp, 1)
    PE.matmul(T.t1_ps[:, 0:128], ident, T.la[:, oa:oa + 128], True, False)
    for i, k in enumerate(others):
        PE.wait_ge(S["arra_%d" % k], n_arr1(k))
        mm = PE.matmul(T.t1_ps[:, 0:128], ident, T.la[:, k * SA:k * SA + 128], False, i == len(others) - 1)
    mm.then_inc(S.t1p, 1)
    for k in others:
        V.wait_ge(S["arra_%d" % k], n_arr1(k))
        A.wait_ge(S["arra_%d" % k], n_arr1(k))
    V.wait_ge(S.negc, 1)
    V.wait_ge(S.scp, 1)
    V.tensor_reduce(T.st2[:, 1:2], T.la[:, A_C::SA], X, AluOpType.min).then_inc(S.nc1, 1)
    A.wait_ge(S.nc1, 1)
    A.activation(T.a1[:], T.la[:, A_C::SA], Exp, bias=T.st2[:, 1:2], scale=-1.0).then_inc(S.a1, 1)
    V.wait_ge(S.a1, 1)
    V.tensor_tensor(T.as1[:], T.a1[:], T.la[:, A_S::SA], mult).then_inc(S.as1, 1)
    V.wait_ge(S.as1, 1)
    V.tensor_reduce(T.st2[:, 0:1], T.as1[:], X, AluOpType.add).then_inc(S.s1, 1)
    V.wait_ge(S.idn, 1)
    for k in [me] + others:
        V.tensor_scalar(T.dg1[:, k * 128:(k + 1) * 128], ident, T.a1[:, k:k + 1], None, mult).then_inc(S["dg1_%d" % k], 1)
    A.wait_ge(S.t1p, 1)
    A.activation(T.tu2[:, 0:128], T.t1_ps[:, 0:128], Copy).then_inc(S.t1c, 1)

    if far:
        m2 = _common_mask(topo, core, far)
        g.wait_ge(S.nc1, 1)
        g.wait_ge(S.s1, 1)
        n_sent += send(far, m2, S.arr2a, T.st2[:, 0:2], T.st2[:, S2:S2 + 2])

    PE.wait_ge(S.ucp, 1)
    for i, k in enumerate([me] + others):
        if k != me:
            PE.wait_ge(S["arrb_%d" % k], n_arr1(k))
        PE.wait_ge(S["dg1_%d" % k], 1)
        mm = PE.matmul(T.u1_ps[:, 0:128], T.dg1[:, k * 128:(k + 1) * 128], T.lb[:, k * SB:(k + 1) * SB], i == 0, i == len(others))
    mm.then_inc(S.u1p, 1)
    V.wait_ge(S.u1p, 1)
    V.tensor_copy(T.tu2[:, 128:256], T.u1_ps[:, 0:128]).then_inc(S.u1c, 1)

    if far:
        g.wait_ge(S.t1c, 1)
        g.wait_ge(S.u1c, 1)
        n_sent += send(far, m2, S.arr2b, T.tu2[:, 0:W2], T.tu2[:, W2:2 * W2])

    V.wait_ge(S.arr2a, n_arr2)
    V.wait_ge(S.nc1, 1)
    V.wait_ge(S.s1, 1)
    V.tensor_reduce(T.nc2[:], T.st2[:, 1::S2], X, AluOpType.min).then_inc(S.nc2, 1)
    A.wait_ge(S.arr2a, n_arr2)
    A.wait_ge(S.nc2, 1)
    A.activation(T.a2[:], T.st2[:, 1::S2], Exp, bias=T.nc2[:], scale=-1.0).then_inc(S.a2, 1)
    V.wait_ge(S.a2, 1)
    V.tensor_tensor(T.as2[:], T.a2[:], T.st2[:, 0::S2], mult).then_inc(S.as2, 1)
    V.wait_ge(S.as2, 1)
    V.tensor_reduce(T.s2[:], T.as2[:], X, AluOpType.add).then_inc(S.s2, 1)
    V.wait_ge(S.s2, 1)
    V.reciprocal(T.rs2[:], T.s2[:]).then_inc(S.rs2, 1)
    V.wait_ge(S.rs2, 1)
    for j in range(2):
        V.tensor_scalar(T.dg2[:, j * 128:(j + 1) * 128], ident, T.a2[:, j:j + 1], T.rs2[:], mult, mult).then_inc(S["dg2_%d" % j], 1)

    PE.wait_ge(S.t1c, 1)
    PE.matmul(T.d_ps[:, 0:128], T.tu2[:, 0:128], ident, True, False)
    PE.wait_ge(S.u1c, 1)
    PE.wait_ge(S.dg2_0, 1)
    PE.matmul(T.d_ps[:, 0:128], T.tu2[:, 128:256], T.dg2[:, 0:128], False, False)
    PE.wait_ge(S.arr2b, n_arr2)
    PE.matmul(T.d_ps[:, 0:128], T.tu2[:, W2:W2 + 128], ident, False, False)
    PE.wait_ge(S.dg2_1, 1)
    PE.matmul(T.d_ps[:, 0:128], T.tu2[:, W2 + 128:W2 + 256], T.dg2[:, 128:256], False, True).then_inc(S.dp, 1)
    V.wait_ge(S.dp, 1)
    V.tensor_copy(T.d_sb[:], T.d_ps[:, 0:128]).then_inc(S.dsb, 1)
    SY.wait_ge(S.dsb, 1)
    SY.dma_start(T.d[:], T.d_sb[:]).then_inc(S.st, 16)
    SY.wait_ge(S.st, 16)
    g.wait_ge(S.sent, n_sent)
